import numpy as np
import ml_dtypes


def mxq(x, axis, fmt="e4m3"):
    dtype, down = {"e4m3": (ml_dtypes.float8_e4m3fn, 7), "e5m2": (ml_dtypes.float8_e5m2, 14)}[fmt]
    v = np.moveaxis(np.asarray(x, np.float32).astype(ml_dtypes.bfloat16).astype(np.float64), axis, -1)
    blocks = v.reshape(v.shape[:-1] + (-1, 32))
    amax = np.abs(blocks).max(-1, keepdims=True)
    byte = np.maximum(np.where(amax > 0, np.frexp(amax)[1] - 1 + 127, 0) - down, 1)
    scale = np.exp2(byte - 127.0)
    codes = (blocks / scale).astype(np.float32).astype(dtype).astype(np.float64)
    return np.moveaxis((codes * scale).reshape(v.shape), -1, axis)


WIDE = False


def mx_kscale(k):
    if not WIDE:
        return np.ones(k)
    levels = np.array([10, -10, 5, -5, 0])
    if k % 512:
        return np.exp2(np.random.permutation(np.resize(levels, k // 32))).repeat(32)
    a = np.empty((k // 512, 16))
    for p in range(k // 512):
        a[p, :8] = np.random.permutation(np.resize(levels, 8))
        for g in range(8):
            far = levels[np.abs(levels - a[p, g]) >= 10]
            a[p, g + 8] = far[np.random.randint(len(far))]
    return np.exp2(a.ravel()).repeat(32)


def f64(x):
    return np.asarray(x).astype(np.float64)


def striped(idx):
    return np.tile(np.asarray(idx).reshape(-1, 16).T, (8, 1)).astype(np.uint16)


def unstriped(offs):
    return offs[:16].T.reshape(-1).astype(np.int64)


E2M1 = np.array([0.0, 0.5, 1.0, 1.5, 2.0, 3.0, 4.0, 6.0, -0.0, -0.5, -1.0, -1.5, -2.0, -3.0, -4.0, -6.0])


def pack_weight(w, fmt):
    k, n = w.shape
    w = f64(np.asarray(w, np.float32).astype(ml_dtypes.bfloat16)).reshape(k // 32, 32, n)
    amax = np.abs(w).max(1)
    if fmt == "e4m3":
        byte = np.frexp(amax)[1] - 1 + 127 - 7
    else:
        mant, ex = np.frexp(amax / 6.0)
        byte = np.where(mant > 0.5, ex, ex - 1) + 127
    byte = np.clip(np.where(amax > 0, byte, 1), 1, 254)
    scaled = (w * np.exp2(127.0 - byte)[:, None, :]).reshape(k, n).astype(np.float32)
    by_word = np.ascontiguousarray(scaled.reshape(k // 512, 128, 4, n).transpose(0, 1, 3, 2))
    if fmt == "e4m3":
        words = by_word.astype(ml_dtypes.float8_e4m3fn).view(np.uint8)
    else:
        c = by_word.astype(ml_dtypes.float4_e2m1fn).view(np.uint8) & 0xF
        words = (c[..., 0::2] | (c[..., 1::2] << 4)).reshape(k // 512, 128, 2 * n)
    return np.ascontiguousarray(words), np.ascontiguousarray(byte.astype(np.uint8).reshape(k // 512, 16, n))


def unpack_weight(words, scales, fmt):
    g, _, n = scales.shape
    words = np.ascontiguousarray(words).reshape(g, 128, n, -1)
    if fmt == "e4m3":
        vals = words.view(ml_dtypes.float8_e4m3fn).astype(np.float64)
    else:
        nib = np.empty((g, 128, n, 4), np.uint8)
        nib[..., 0::2] = words & 0xF
        nib[..., 1::2] = words >> 4
        vals = E2M1[nib]
    vals = vals * np.repeat(np.exp2(scales.astype(np.float64) - 127.0), 8, axis=1)[..., None]
    return vals.transpose(0, 1, 3, 2).reshape(g * 512, n)


def sigmoid(v):
    return 1.0 / (1.0 + np.exp(-v))


K, T, L, J, N = 1024, 512, 512, 512, 512


def setup_inputs():
    n = np.random.standard_normal
    idx = np.random.randint(0, T, J)
    fk = mx_kscale(K)
    fl = mx_kscale(L)
    xtp = pack_weight(n((K, T)) / fk[:, None], "e2m1")
    wp = pack_weight(n((K, N)) * 1 / np.sqrt(K) * fk[:, None], "e4m3")
    wrp = pack_weight(n((L, N)) * 1 / np.sqrt(L) * fl[:, None], "e2m1")
    wgp = pack_weight(n((L, N)) * 1 / np.sqrt(L) * fl[:, None], "e4m3")
    return {
        "xt_words": xtp[0],
        "xt_scales": xtp[1],
        "w_words": wp[0],
        "w_scales": wp[1],
        "rq": (n((L, J)) / fl[:, None]).astype(np.float32),
        "wr_words": wrp[0],
        "wr_scales": wrp[1],
        "wg_words": wgp[0],
        "wg_scales": wgp[1],
        "offs": striped(idx),
    }


def reference(xt_words, xt_scales, w_words, w_scales, rq, wr_words, wr_scales, wg_words, wg_scales, offs):
    idx = unstriped(offs)
    xtu = unpack_weight(xt_words, xt_scales, "e2m1")
    wu = unpack_weight(w_words, w_scales, "e4m3")
    wru = unpack_weight(wr_words, wr_scales, "e2m1")
    wgu = unpack_weight(wg_words, wg_scales, "e4m3")
    z = wu.T @ xtu
    rqq = mxq(f64(rq), 0, "e4m3")
    r = wru.T @ rqq
    g = wgu.T @ rqq
    y = r + sigmoid(g) * (z[:, idx] - r)
    return y

@@ -1,0 +1,162 @@
+from contextlib import ExitStack
+
+import concourse.mybir as mybir
+
+K, T, L, J, N = 1024, 512, 512, 512, 512
+FLOPS = 2 * N * (K * T + 2 * L * J)
+
+F32 = mybir.dt.float32
+BF16 = mybir.dt.bfloat16
+I32 = mybir.dt.int32
+U32 = mybir.dt.uint32
+U16 = mybir.dt.uint16
+U8 = mybir.dt.uint8
+FP8X4 = mybir.dt.float8_e4m3fn_x4
+FP4X4 = mybir.dt.float4_e2m1fn_x4
+ALU = mybir.AluOpType
+ACT = mybir.ActivationFunctionType
+
+P = 128
+PACK = 4
+HALF = J // 2
+TILES = N // P
+PASSES = K // (P * PACK)
+WG, WR, XT, W = 0, 1, 2, 4
+PLANES = 6
+
+
+def tile_list_blended_readout_kernel(
+    tc, xt_words, xt_scales, w_words, w_scales, rq, wr_words, wr_scales, wg_words, wg_scales, offs, out
+):
+    nc = tc.nc
+    with ExitStack() as ctx:
+        keep = ctx.enter_context(tc.tile_pool(name="keep", bufs=1))
+        psum = ctx.enter_context(tc.psum_pool(name="psum", bufs=1))
+
+        offsets = keep.tile([P, J // 16], U16, name="offsets")
+        nc.sync.dma_start(offsets[:], offs)
+
+        staged = keep.tile([16, PLANES * N], U8, name="staged")
+        for first, count, src in ((WG, 1, wg_scales), (WR, 1, wr_scales), (XT, PASSES, xt_scales), (W, PASSES, w_scales)):
+            nc.sync.dma_start(
+                staged[:, first * N : (first + count) * N].bitcast(I32).rearrange("q (z c) -> q z c", z=count),
+                src.bitcast(I32).rearrange("z q c -> q z c"),
+            )
+
+        rq_rows = rq.rearrange("(p t) j -> p t j", t=PACK)
+        raw = []
+        for h in range(2):
+            raw_h = keep.tile([P, PACK, HALF], F32, name="raw%d" % h, tag="raw%d" % h, align_bytes=64)
+            nc.sync.dma_start(raw_h[:], rq_rows[:, :, h * HALF : (h + 1) * HALF])
+            raw.append(raw_h)
+
+        wg = keep.tile([P, N], U32, name="wg", align_bytes=64)
+        nc.sync.dma_start(wg[:].bitcast(I32), wg_words[0].rearrange("p n t -> p (n t)").bitcast(I32))
+        wr = keep.tile([P, 2 * N], U8, name="wr", align_bytes=64)
+        nc.sync.dma_start(wr[:].bitcast(I32), wr_words[0].bitcast(I32))
+        xt = keep.tile([P, PASSES, 2 * T], U8, name="xt", align_bytes=64)
+        nc.sync.dma_start(xt[:].bitcast(I32), xt_words.bitcast(I32).rearrange("z p c -> p z c"))
+
+        planes = keep.tile([P, PLANES * N], U8, name="planes", align_bytes=64)
+        nc.vector.memset(planes[:].bitcast(U32), 0)
+        warm = keep.tile([P, 2], F32, name="warm")
+        nc.gpsimd.memset(warm[:, 0:1], 0.0)
+        nc.scalar.activation(warm[:, 1:2], warm[:, 0:1], ACT.Sigmoid)
+        for q in range(4):
+            nc.scalar.dma_start(planes[32 * q : 32 * q + 4, :].bitcast(I32), staged[4 * q : 4 * q + 4, :].bitcast(I32))
+
+        rq_codes = keep.tile([P, J], U32, name="rq_codes", align_bytes=64)
+        rq_plane = keep.tile([P, J], U8, name="rq_plane", align_bytes=64)
+        for h in range(2):
+            grouped = keep.tile([P, HALF, PACK], BF16, name="grouped%d" % h, align_bytes=64)
+            nc.vector.tensor_copy(
+                grouped[:].rearrange("p (c i) t -> p c t i", i=4), raw[h][:].rearrange("p t (c i) -> p c t i", i=4)
+            )
+            cols = slice(h * HALF, (h + 1) * HALF)
+            nc.vector.quantize_mx(
+                out=rq_codes[:, cols].bitcast(FP8X4),
+                scales=rq_plane[:, cols],
+                in_=grouped[:].rearrange("p c t -> p (c t)"),
+            )
+
+        w = keep.tile([P, PASSES, N], U32, name="w", tag="raw0", align_bytes=64)
+        nc.sync.dma_start(w[:].bitcast(I32), w_words.rearrange("z p n t -> p z (n t)").bitcast(I32))
+
+        def scale_cols(plane, first, count):
+            return planes[:, plane * N + first : plane * N + first + count]
+
+        gate, own, book = [], [], []
+
+        def request_side(i):
+            g_acc = psum.tile([P, J], F32, name="g_acc", tag="g", bufs=2)
+            nc.tensor.matmul_mx(
+                out=g_acc[:],
+                lhsT=wg[:, i * P : (i + 1) * P].bitcast(FP8X4),
+                lhsT_scale=scale_cols(WG, i * P, P),
+                rhs=rq_codes[:].bitcast(FP8X4),
+                rhs_scale=rq_plane[:],
+                start=True,
+                stop=True,
+            )
+            r_acc = psum.tile([P, J], F32, name="r_acc", tag="r", bufs=3)
+            nc.tensor.matmul_mx(
+                out=r_acc[:],
+                lhsT=wr[:, 2 * i * P : 2 * (i + 1) * P].bitcast(FP4X4),
+                lhsT_scale=scale_cols(WR, i * P, P),
+                rhs=rq_codes[:].bitcast(FP8X4),
+                rhs_scale=rq_plane[:],
+                start=True,
+                stop=True,
+            )
+            s = keep.tile([P, J], F32, name="s%d" % i)
+            nc.scalar.activation(s[:], g_acc[:], ACT.Sigmoid)
+            v = keep.tile([P, J], F32, name="v%d" % i)
+            nc.vector.scalar_tensor_tensor(v[:], s[:], 1.0, r_acc[:], ALU.subtract, ALU.mult)
+            gate.append(s)
+            own.append(v)
+
+        def book_side(i):
+            z_acc = psum.tile([P, T], F32, name="z_acc", tag="z", bufs=3)
+            for z in range(PASSES):
+                nc.tensor.matmul_mx(
+                    out=z_acc[:],
+                    lhsT=w[:, z, i * P : (i + 1) * P].bitcast(FP8X4),
+                    lhsT_scale=scale_cols(W + z, i * P, P),
+                    rhs=xt[:, z, :].bitcast(FP4X4),
+                    rhs_scale=scale_cols(XT + z, 0, T),
+                    start=(z == 0),
+                    stop=(z == PASSES - 1),
+                )
+            table = keep.tile([P, T], F32, name="table%d" % i)
+            nc.scalar.copy(table[:], z_acc[:])
+            book.append(table)
+
+        picked = []
+
+        def look_up(i):
+            t = keep.tile([P, J], F32, name="t%d" % i)
+            for h in range(2):
+                cols = slice(h * HALF, (h + 1) * HALF)
+                nc.vector.tensor_tensor(
+                    t[:, cols], book[i][:].indirect(offsets[:, h * HALF // 16 : (h + 1) * HALF // 16]), gate[i][:, cols], ALU.mult
+                )
+            picked.append(t)
+
+        def finish(i, first, count):
+            cols = slice(first, first + count)
+            y = keep.tile([P, count], F32, name="y%d_%d" % (i, first))
+            nc.vector.tensor_tensor(y[:], picked[i][:, cols], own[i][:, cols], ALU.subtract)
+            nc.sync.dma_start(out[i * P : (i + 1) * P, cols], y[:])
+
+        request_side(0)
+        request_side(1)
+        for i in range(TILES):
+            book_side(i)
+            if i + 2 < TILES:
+                request_side(i + 2)
+        for i in range(TILES):
+            look_up(i)
+            if i > 0:
+                finish(i - 1, 0, J)
+        finish(TILES - 1, 0, HALF)
+        finish(TILES - 1, HALF, HALF)

@@ -1,6 +1,7 @@
 from contextlib import ExitStack
 
 import concourse.mybir as mybir
+from concourse.masks import make_identity
 
 K, T, L, J, N = 1024, 512, 512, 512, 512
 FLOPS = 2 * N * (K * T + 2 * L * J)
@@ -19,10 +20,16 @@ ACT = mybir.ActivationFunctionType
 P = 128
 PACK = 4
 HALF = J // 2
-TILES = N // P
+UNIT = 2 * HALF
 PASSES = K // (P * PACK)
-WG, WR, XT, W = 0, 1, 2, 4
-PLANES = 6
+QUADRANTS = 4
+STRIPE = 16
+
+G_BANK = {(0, 0): "a", (1, 0): "c", (0, 1): "a", (1, 1): "f"}
+R_BANK = {(0, 0): "b", (1, 0): "d", (0, 1): "e", (1, 1): "g"}
+Z_BANK = ["f", "g", "h", "c"]
+TURNED_BANK = ["h", "c"]
+BACK_BANK = ["a", "b"]
 
 
 def tile_list_blended_readout_kernel(
@@ -33,130 +40,204 @@ def tile_list_blended_readout_kernel(
         keep = ctx.enter_context(tc.tile_pool(name="keep", bufs=1))
         psum = ctx.enter_context(tc.psum_pool(name="psum", bufs=1))
 
-        offsets = keep.tile([P, J // 16], U16, name="offsets")
-        nc.sync.dma_start(offsets[:], offs)
+        def plane_rows(q):
+            return slice(32 * q, 32 * q + 4)
 
-        staged = keep.tile([16, PLANES * N], U8, name="staged")
-        for first, count, src in ((WG, 1, wg_scales), (WR, 1, wr_scales), (XT, PASSES, xt_scales), (W, PASSES, w_scales)):
-            nc.sync.dma_start(
-                staged[:, first * N : (first + count) * N].bitcast(I32).rearrange("q (z c) -> q z c", z=count),
-                src.bitcast(I32).rearrange("z q c -> q z c"),
-            )
+        def scale_rows(q):
+            return slice(4 * q, 4 * q + 4)
+
+        wg_landed = keep.tile([P, N], U8, name="wg_landed")
+        wr_landed = keep.tile([P, N], U8, name="wr_landed")
+
+        def load_scale_rows(queue, landed, scales, q):
+            queue.dma_start(landed[plane_rows(q), :].bitcast(I32), scales[0, scale_rows(q), :].bitcast(I32))
+
+        for q in range(QUADRANTS - 1):
+            load_scale_rows(nc.sync, wg_landed, wg_scales, q)
+        load_scale_rows(nc.scalar, wg_landed, wg_scales, QUADRANTS - 1)
+        for q in range(QUADRANTS // 2):
+            load_scale_rows(nc.scalar, wr_landed, wr_scales, q)
 
         rq_rows = rq.rearrange("(p t) j -> p t j", t=PACK)
-        raw = []
-        for h in range(2):
-            raw_h = keep.tile([P, PACK, HALF], F32, name="raw%d" % h, tag="raw%d" % h, align_bytes=64)
-            nc.sync.dma_start(raw_h[:], rq_rows[:, :, h * HALF : (h + 1) * HALF])
-            raw.append(raw_h)
-
+        raw = [keep.tile([P, PACK, HALF], F32, name="raw%d" % h, tag="raw%d" % h, align_bytes=64) for h in range(2)]
+        nc.sync.dma_start(raw[0][:], rq_rows[:, :, 0:HALF])
         wg = keep.tile([P, N], U32, name="wg", align_bytes=64)
         nc.sync.dma_start(wg[:].bitcast(I32), wg_words[0].rearrange("p n t -> p (n t)").bitcast(I32))
+        for q in range(QUADRANTS // 2, QUADRANTS):
+            load_scale_rows(nc.sync, wr_landed, wr_scales, q)
         wr = keep.tile([P, 2 * N], U8, name="wr", align_bytes=64)
         nc.sync.dma_start(wr[:].bitcast(I32), wr_words[0].bitcast(I32))
+
+        staged = keep.tile([16, 2 * PASSES * N], U8, name="staged")
+        for first, scales in ((0, xt_scales), (PASSES, w_scales)):
+            nc.sync.dma_start(
+                staged[:, first * N : (first + PASSES) * N].bitcast(I32).rearrange("q (z c) -> q z c", z=PASSES),
+                scales.bitcast(I32).rearrange("z q c -> q z c"),
+            )
+        nc.sync.dma_start(raw[1][:], rq_rows[:, :, HALF:J])
         xt = keep.tile([P, PASSES, 2 * T], U8, name="xt", align_bytes=64)
         nc.sync.dma_start(xt[:].bitcast(I32), xt_words.bitcast(I32).rearrange("z p c -> p z c"))
+        w_view = w_words.rearrange("z p n t -> p z (n t)").bitcast(I32)
+        w = [keep.tile([P, PASSES, 2 * P], U32, name="w0", align_bytes=64)]
+        nc.sync.dma_start(w[0][:].bitcast(I32), w_view[:, :, 0 : 2 * P])
+        offsets = keep.tile([P, J // STRIPE], U16, name="offsets")
+        nc.sync.dma_start(offsets[:], offs)
 
-        planes = keep.tile([P, PLANES * N], U8, name="planes", align_bytes=64)
-        nc.vector.memset(planes[:].bitcast(U32), 0)
+        wg_plane = keep.tile([P, N], U8, name="wg_plane", align_bytes=64)
+        wr_plane = keep.tile([P, N], U8, name="wr_plane", align_bytes=64)
+        book_planes = keep.tile([P, 2 * PASSES * N], U8, name="book_planes", align_bytes=64)
         warm = keep.tile([P, 2], F32, name="warm")
         nc.gpsimd.memset(warm[:, 0:1], 0.0)
         nc.scalar.activation(warm[:, 1:2], warm[:, 0:1], ACT.Sigmoid)
-        for q in range(4):
-            nc.scalar.dma_start(planes[32 * q : 32 * q + 4, :].bitcast(I32), staged[4 * q : 4 * q + 4, :].bitcast(I32))
+        for plane in (wg_plane, wr_plane, book_planes):
+            nc.vector.memset(plane[:].bitcast(U32), 0)
+        ident = keep.tile([P, P], F32, name="ident")
+        make_identity(nc, ident[:])
+        for plane, landed in ((wg_plane, wg_landed), (wr_plane, wr_landed)):
+            for q in range(QUADRANTS):
+                nc.gpsimd.tensor_copy(plane[plane_rows(q), :].bitcast(I32), landed[plane_rows(q), :].bitcast(I32))
+        for q in range(QUADRANTS):
+            nc.scalar.dma_start(book_planes[plane_rows(q), :].bitcast(I32), staged[scale_rows(q), :].bitcast(I32))
 
-        rq_codes = keep.tile([P, J], U32, name="rq_codes", align_bytes=64)
-        rq_plane = keep.tile([P, J], U8, name="rq_plane", align_bytes=64)
-        for h in range(2):
+        rq_codes, rq_planes = [], []
+
+        def quantise(h):
             grouped = keep.tile([P, HALF, PACK], BF16, name="grouped%d" % h, align_bytes=64)
-            nc.vector.tensor_copy(
-                grouped[:].rearrange("p (c i) t -> p c t i", i=4), raw[h][:].rearrange("p t (c i) -> p c t i", i=4)
+            nc.vector.tensor_scalar(
+                grouped[:].rearrange("p (c i) t -> p c t i", i=4),
+                raw[h][:].rearrange("p t (c i) -> p c t i", i=4),
+                -1.0,
+                None,
+                ALU.mult,
             )
-            cols = slice(h * HALF, (h + 1) * HALF)
+            codes = keep.tile([P, HALF], U32, name="rq_codes%d" % h, align_bytes=64)
+            plane = keep.tile([P, HALF], U8, name="rq_plane%d" % h, align_bytes=64)
             nc.vector.quantize_mx(
-                out=rq_codes[:, cols].bitcast(FP8X4),
-                scales=rq_plane[:, cols],
-                in_=grouped[:].rearrange("p c t -> p (c t)"),
+                out=codes[:].bitcast(FP8X4), scales=plane[:], in_=grouped[:].rearrange("p c t -> p (c t)")
             )
+            rq_codes.append(codes)
+            rq_planes.append(plane)
 
-        w = keep.tile([P, PASSES, N], U32, name="w", tag="raw0", align_bytes=64)
-        nc.sync.dma_start(w[:].bitcast(I32), w_words.rearrange("z p n t -> p z (n t)").bitcast(I32))
+        gate, minus_r, own_term, book, book_term, turned = {}, {}, {}, {}, {}, {}
 
-        def scale_cols(plane, first, count):
-            return planes[:, plane * N + first : plane * N + first + count]
+        def request_side(pair, h):
+            g_acc = psum.tile([P, 2, HALF], F32, name="g_acc", tag=G_BANK[pair, h])
+            for a in range(2):
+                n0 = (2 * pair + a) * P
+                nc.tensor.matmul_mx(
+                    out=g_acc[:, a, :],
+                    lhsT=wg[:, n0 : n0 + P].bitcast(FP8X4),
+                    lhsT_scale=wg_plane[:, n0 : n0 + P],
+                    rhs=rq_codes[h][:].bitcast(FP8X4),
+                    rhs_scale=rq_planes[h][:],
+                    start=True,
+                    stop=True,
+                )
+            r_acc = psum.tile([P, 2, HALF], F32, name="r_acc", tag=R_BANK[pair, h])
+            for a in range(2):
+                n0 = (2 * pair + a) * P
+                nc.tensor.matmul_mx(
+                    out=r_acc[:, a, :],
+                    lhsT=wr[:, 2 * n0 : 2 * (n0 + P)].bitcast(FP4X4),
+                    lhsT_scale=wr_plane[:, n0 : n0 + P],
+                    rhs=rq_codes[h][:].bitcast(FP8X4),
+                    rhs_scale=rq_planes[h][:],
+                    start=True,
+                    stop=True,
+                )
+            s = keep.tile([P, UNIT], F32, name="s%d_%d" % (pair, h), tag="s%d_%d" % (pair, h))
+            nc.scalar.activation(s[:], g_acc[:].rearrange("p a j -> p (a j)"), ACT.Sigmoid, scale=-1.0)
+            gate[pair, h] = s
+            minus_r[pair, h] = r_acc
 
-        gate, own, book = [], [], []
-
-        def request_side(i):
-            g_acc = psum.tile([P, J], F32, name="g_acc", tag="g", bufs=2)
-            nc.tensor.matmul_mx(
-                out=g_acc[:],
-                lhsT=wg[:, i * P : (i + 1) * P].bitcast(FP8X4),
-                lhsT_scale=scale_cols(WG, i * P, P),
-                rhs=rq_codes[:].bitcast(FP8X4),
-                rhs_scale=rq_plane[:],
-                start=True,
-                stop=True,
+        def weigh_own(pair, h, tag):
+            v = keep.tile([P, UNIT], F32, name="v%d_%d" % (pair, h), tag=tag)
+            nc.vector.scalar_tensor_tensor(
+                v[:], gate[pair, h][:], 1.0, minus_r[pair, h][:].rearrange("p a j -> p (a j)"), ALU.subtract, ALU.mult
             )
-            r_acc = psum.tile([P, J], F32, name="r_acc", tag="r", bufs=3)
-            nc.tensor.matmul_mx(
-                out=r_acc[:],
-                lhsT=wr[:, 2 * i * P : 2 * (i + 1) * P].bitcast(FP4X4),
-                lhsT_scale=scale_cols(WR, i * P, P),
-                rhs=rq_codes[:].bitcast(FP8X4),
-                rhs_scale=rq_plane[:],
-                start=True,
-                stop=True,
-            )
-            s = keep.tile([P, J], F32, name="s%d" % i)
-            nc.scalar.activation(s[:], g_acc[:], ACT.Sigmoid)
-            v = keep.tile([P, J], F32, name="v%d" % i)
-            nc.vector.scalar_tensor_tensor(v[:], s[:], 1.0, r_acc[:], ALU.subtract, ALU.mult)
-            gate.append(s)
-            own.append(v)
+            own_term[pair, h] = v
 
         def book_side(i):
-            z_acc = psum.tile([P, T], F32, name="z_acc", tag="z", bufs=3)
+            z_acc = psum.tile([P, T], F32, name="z_acc", tag=Z_BANK[i])
+            a = i % 2
             for z in range(PASSES):
+                w_col = (PASSES + z) * N + i * P
                 nc.tensor.matmul_mx(
                     out=z_acc[:],
-                    lhsT=w[:, z, i * P : (i + 1) * P].bitcast(FP8X4),
-                    lhsT_scale=scale_cols(W + z, i * P, P),
+                    lhsT=w[i // 2][:, z, a * P : (a + 1) * P].bitcast(FP8X4),
+                    lhsT_scale=book_planes[:, w_col : w_col + P],
                     rhs=xt[:, z, :].bitcast(FP4X4),
-                    rhs_scale=scale_cols(XT + z, 0, T),
+                    rhs_scale=book_planes[:, z * T : (z + 1) * T],
                     start=(z == 0),
                     stop=(z == PASSES - 1),
                 )
             table = keep.tile([P, T], F32, name="table%d" % i)
             nc.scalar.copy(table[:], z_acc[:])
-            book.append(table)
+            book[i] = table
 
-        picked = []
-
-        def look_up(i):
-            t = keep.tile([P, J], F32, name="t%d" % i)
-            for h in range(2):
-                cols = slice(h * HALF, (h + 1) * HALF)
+        def look_up(pair, h):
+            picked = keep.tile([P, UNIT], F32, name="picked%d_%d" % (pair, h))
+            for a in range(2):
+                cols = slice(a * HALF, (a + 1) * HALF)
                 nc.vector.tensor_tensor(
-                    t[:, cols], book[i][:].indirect(offsets[:, h * HALF // 16 : (h + 1) * HALF // 16]), gate[i][:, cols], ALU.mult
+                    picked[:, cols],
+                    book[2 * pair + a][:].indirect(offsets[:, h * HALF // STRIPE : (h + 1) * HALF // STRIPE]),
+                    gate[pair, h][:, cols],
+                    ALU.mult,
                 )
-            picked.append(t)
+            book_term[pair, h] = picked
 
-        def finish(i, first, count):
-            cols = slice(first, first + count)
-            y = keep.tile([P, count], F32, name="y%d_%d" % (i, first))
-            nc.vector.tensor_tensor(y[:], picked[i][:, cols], own[i][:, cols], ALU.subtract)
-            nc.sync.dma_start(out[i * P : (i + 1) * P, cols], y[:])
+        def out_view(pair, h):
+            return out[2 * pair * P : 2 * (pair + 1) * P, h * HALF : (h + 1) * HALF].rearrange("(a p) j -> p a j", p=P)
 
-        request_side(0)
-        request_side(1)
-        for i in range(TILES):
-            book_side(i)
-            if i + 2 < TILES:
-                request_side(i + 2)
-        for i in range(TILES):
-            look_up(i)
-            if i > 0:
-                finish(i - 1, 0, J)
-        finish(TILES - 1, 0, HALF)
-        finish(TILES - 1, HALF, HALF)
+        def add_on_vector(h, a0, a1):
+            cols = slice(a0 * HALF, a1 * HALF)
+            y = keep.tile([P, a1 - a0, HALF], F32, name="y1_%d_%d" % (h, a0))
+            nc.vector.tensor_tensor(
+                y[:].rearrange("p a j -> p (a j)"), book_term[1, h][:, cols], own_term[1, h][:, cols], ALU.add
+            )
+            nc.sync.dma_start(out_view(1, h)[:, a0:a1, :], y[:])
+
+        blocks = [slice(b * P, (b + 1) * P) for b in range(UNIT // P)]
+
+        def add_turned(h):
+            turned_acc = psum.tile([P, UNIT], F32, name="turned_acc", tag=TURNED_BANK[h])
+            terms = [(term, cols) for term in (own_term[0, h], book_term[0, h]) for cols in blocks]
+            for n, (term, cols) in enumerate(terms):
+                nc.tensor.matmul(
+                    turned_acc[:, cols], term[:, cols], ident[:], start=(n == 0), stop=(n == len(terms) - 1), is_transpose=True
+                )
+            turned[h] = keep.tile([P, UNIT], F32, name="turned%d" % h)
+            nc.scalar.copy(turned[h][:], turned_acc[:])
+
+        def turn_back(h):
+            back_acc = psum.tile([P, UNIT], F32, name="back_acc", tag=BACK_BANK[h])
+            for cols in blocks:
+                nc.tensor.transpose(back_acc[:, cols], turned[h][:, cols], ident[:])
+            y = keep.tile([P, 2, HALF], F32, name="y0_%d" % h, tag="v0_%d" % (1 - h))
+            nc.scalar.copy(y[:].rearrange("p a j -> p (a j)"), back_acc[:])
+            nc.scalar.dma_start(out_view(0, h), y[:])
+
+        quantise(0)
+        quantise(1)
+        w.append(keep.tile([P, PASSES, 2 * P], U32, name="w1", tag="raw1", align_bytes=64))
+        nc.sync.dma_start(w[1][:].bitcast(I32), w_view[:, :, 2 * P : 4 * P])
+        for pair, h in ((0, 0), (1, 0), (0, 1)):
+            request_side(pair, h)
+            weigh_own(pair, h, "v%d_%d" % (pair, h))
+        book_side(0)
+        book_side(1)
+        request_side(1, 1)
+        book_side(2)
+        book_side(3)
+        for h in range(2):
+            look_up(0, h)
+            add_turned(h)
+        for h in range(2):
+            turn_back(h)
+        look_up(1, 0)
+        weigh_own(1, 1, "s0_1")
+        add_on_vector(0, 0, 2)
+        look_up(1, 1)
+        add_on_vector(1, 0, 1)
+        add_on_vector(1, 1, 2)

@@ -21,6 +21,7 @@ P = 128
 PACK = 4
 HALF = J // 2
 UNIT = 2 * HALF
+PIECE = HALF // 2
 PASSES = K // (P * PACK)
 QUADRANTS = 4
 STRIPE = 16
@@ -102,37 +103,44 @@ def tile_list_blended_readout_kernel(
         rq_codes, rq_planes = [], []
 
         def quantise(h):
-            grouped = keep.tile([P, HALF, PACK], BF16, name="grouped%d" % h, align_bytes=64)
-            nc.vector.tensor_scalar(
-                grouped[:].rearrange("p (c i) t -> p c t i", i=4),
-                raw[h][:].rearrange("p t (c i) -> p c t i", i=4),
-                -1.0,
-                None,
-                ALU.mult,
-            )
             codes = keep.tile([P, HALF], U32, name="rq_codes%d" % h, align_bytes=64)
             plane = keep.tile([P, HALF], U8, name="rq_plane%d" % h, align_bytes=64)
-            nc.vector.quantize_mx(
-                out=codes[:].bitcast(FP8X4), scales=plane[:], in_=grouped[:].rearrange("p c t -> p (c t)")
-            )
+            pieces = [slice(c0, c0 + PIECE) for c0 in range(0, HALF, PIECE)]
+            grouped = [
+                keep.tile([P, PIECE, PACK], BF16, name="grouped%d_%d" % (h, n), align_bytes=64) for n in range(len(pieces))
+            ]
+            for cols, dst in zip(pieces, grouped):
+                nc.vector.tensor_scalar(
+                    dst[:].rearrange("p (c i) t -> p c t i", i=4),
+                    raw[h][:, :, cols].rearrange("p t (c i) -> p c t i", i=4),
+                    -1.0,
+                    None,
+                    ALU.mult,
+                )
+            for cols, src in zip(pieces, grouped):
+                nc.vector.quantize_mx(
+                    out=codes[:, cols].bitcast(FP8X4), scales=plane[:, cols], in_=src[:].rearrange("p c t -> p (c t)")
+                )
             rq_codes.append(codes)
             rq_planes.append(plane)
 
         gate, minus_r, own_term, book, book_term, turned = {}, {}, {}, {}, {}, {}
 
-        def request_side(pair, h):
+        def request_side(pair, h, g_width):
             g_acc = psum.tile([P, 2, HALF], F32, name="g_acc", tag=G_BANK[pair, h])
-            for a in range(2):
-                n0 = (2 * pair + a) * P
-                nc.tensor.matmul_mx(
-                    out=g_acc[:, a, :],
-                    lhsT=wg[:, n0 : n0 + P].bitcast(FP8X4),
-                    lhsT_scale=wg_plane[:, n0 : n0 + P],
-                    rhs=rq_codes[h][:].bitcast(FP8X4),
-                    rhs_scale=rq_planes[h][:],
-                    start=True,
-                    stop=True,
-                )
+            for c0 in range(0, HALF, g_width):
+                cols = slice(c0, c0 + g_width)
+                for a in range(2):
+                    n0 = (2 * pair + a) * P
+                    nc.tensor.matmul_mx(
+                        out=g_acc[:, a, cols],
+                        lhsT=wg[:, n0 : n0 + P].bitcast(FP8X4),
+                        lhsT_scale=wg_plane[:, n0 : n0 + P],
+                        rhs=rq_codes[h][:, cols].bitcast(FP8X4),
+                        rhs_scale=rq_planes[h][:, cols],
+                        start=True,
+                        stop=True,
+                    )
             r_acc = psum.tile([P, 2, HALF], F32, name="r_acc", tag=R_BANK[pair, h])
             for a in range(2):
                 n0 = (2 * pair + a) * P
@@ -222,12 +230,12 @@ def tile_list_blended_readout_kernel(
         quantise(1)
         w.append(keep.tile([P, PASSES, 2 * P], U32, name="w1", tag="raw1", align_bytes=64))
         nc.sync.dma_start(w[1][:].bitcast(I32), w_view[:, :, 2 * P : 4 * P])
-        for pair, h in ((0, 0), (1, 0), (0, 1)):
-            request_side(pair, h)
+        for pair, h, g_width in ((0, 0, PIECE), (1, 0, HALF), (0, 1, HALF)):
+            request_side(pair, h, g_width)
             weigh_own(pair, h, "v%d_%d" % (pair, h))
         book_side(0)
         book_side(1)
-        request_side(1, 1)
+        request_side(1, 1, HALF)
         book_side(2)
         book_side(3)
         for h in range(2):

from contextlib import ExitStack

import concourse.mybir as mybir
from concourse.masks import make_identity

K, T, L, J, N = 1024, 512, 512, 512, 512
FLOPS = 2 * N * (K * T + 2 * L * J)

F32 = mybir.dt.float32
BF16 = mybir.dt.bfloat16
I32 = mybir.dt.int32
U32 = mybir.dt.uint32
U16 = mybir.dt.uint16
U8 = mybir.dt.uint8
FP8X4 = mybir.dt.float8_e4m3fn_x4
FP4X4 = mybir.dt.float4_e2m1fn_x4
ALU = mybir.AluOpType
ACT = mybir.ActivationFunctionType

P = 128
PACK = 4
HALF = J // 2
UNIT = 2 * HALF
PIECE = HALF // 2
PASSES = K // (P * PACK)
QUADRANTS = 4
STRIPE = 16

G_BANK = {(0, 0): "a", (1, 0): "c", (0, 1): "a", (1, 1): "f"}
R_BANK = {(0, 0): "b", (1, 0): "d", (0, 1): "e", (1, 1): "g"}
Z_BANK = ["f", "g", "h", "c"]
TURNED_BANK = ["h", "c"]
BACK_BANK = ["a", "b"]


def tile_list_blended_readout_kernel(
    tc, xt_words, xt_scales, w_words, w_scales, rq, wr_words, wr_scales, wg_words, wg_scales, offs, out
):
    nc = tc.nc
    with ExitStack() as ctx:
        keep = ctx.enter_context(tc.tile_pool(name="keep", bufs=1))
        psum = ctx.enter_context(tc.psum_pool(name="psum", bufs=1))

        def plane_rows(q):
            return slice(32 * q, 32 * q + 4)

        def scale_rows(q):
            return slice(4 * q, 4 * q + 4)

        wg_landed = keep.tile([P, N], U8, name="wg_landed")
        wr_landed = keep.tile([P, N], U8, name="wr_landed")

        def load_scale_rows(queue, landed, scales, q):
            queue.dma_start(landed[plane_rows(q), :].bitcast(I32), scales[0, scale_rows(q), :].bitcast(I32))

        for q in range(QUADRANTS - 1):
            load_scale_rows(nc.sync, wg_landed, wg_scales, q)
        load_scale_rows(nc.scalar, wg_landed, wg_scales, QUADRANTS - 1)
        for q in range(QUADRANTS // 2):
            load_scale_rows(nc.scalar, wr_landed, wr_scales, q)

        rq_rows = rq.rearrange("(p t) j -> p t j", t=PACK)
        raw = [keep.tile([P, PACK, HALF], F32, name="raw%d" % h, tag="raw%d" % h, align_bytes=64) for h in range(2)]
        nc.sync.dma_start(raw[0][:], rq_rows[:, :, 0:HALF])
        wg = keep.tile([P, N], U32, name="wg", align_bytes=64)
        nc.sync.dma_start(wg[:].bitcast(I32), wg_words[0].rearrange("p n t -> p (n t)").bitcast(I32))
        for q in range(QUADRANTS // 2, QUADRANTS):
            load_scale_rows(nc.sync, wr_landed, wr_scales, q)
        wr = keep.tile([P, 2 * N], U8, name="wr", align_bytes=64)
        nc.sync.dma_start(wr[:].bitcast(I32), wr_words[0].bitcast(I32))

        staged = keep.tile([16, 2 * PASSES * N], U8, name="staged")
        for first, scales in ((0, xt_scales), (PASSES, w_scales)):
            nc.sync.dma_start(
                staged[:, first * N : (first + PASSES) * N].bitcast(I32).rearrange("q (z c) -> q z c", z=PASSES),
                scales.bitcast(I32).rearrange("z q c -> q z c"),
            )
        nc.sync.dma_start(raw[1][:], rq_rows[:, :, HALF:J])
        xt = keep.tile([P, PASSES, 2 * T], U8, name="xt", align_bytes=64)
        nc.sync.dma_start(xt[:].bitcast(I32), xt_words.bitcast(I32).rearrange("z p c -> p z c"))
        w_view = w_words.rearrange("z p n t -> p z (n t)").bitcast(I32)
        w = [keep.tile([P, PASSES, 2 * P], U32, name="w0", align_bytes=64)]
        nc.sync.dma_start(w[0][:].bitcast(I32), w_view[:, :, 0 : 2 * P])
        offsets = keep.tile([P, J // STRIPE], U16, name="offsets")
        nc.sync.dma_start(offsets[:], offs)

        wg_plane = keep.tile([P, N], U8, name="wg_plane", align_bytes=64)
        wr_plane = keep.tile([P, N], U8, name="wr_plane", align_bytes=64)
        book_planes = keep.tile([P, 2 * PASSES * N], U8, name="book_planes", align_bytes=64)
        warm = keep.tile([P, 2], F32, name="warm")
        nc.gpsimd.memset(warm[:, 0:1], 0.0)
        nc.scalar.activation(warm[:, 1:2], warm[:, 0:1], ACT.Sigmoid)
        for plane in (wg_plane, wr_plane, book_planes):
            nc.vector.memset(plane[:].bitcast(U32), 0)
        ident = keep.tile([P, P], F32, name="ident")
        make_identity(nc, ident[:])
        for plane, landed in ((wg_plane, wg_landed), (wr_plane, wr_landed)):
            for q in range(QUADRANTS):
                nc.gpsimd.tensor_copy(plane[plane_rows(q), :].bitcast(I32), landed[plane_rows(q), :].bitcast(I32))
        for q in range(QUADRANTS):
            nc.scalar.dma_start(book_planes[plane_rows(q), :].bitcast(I32), staged[scale_rows(q), :].bitcast(I32))

        rq_codes, rq_planes = [], []

        def quantise(h):
            codes = keep.tile([P, HALF], U32, name="rq_codes%d" % h, align_bytes=64)
            plane = keep.tile([P, HALF], U8, name="rq_plane%d" % h, align_bytes=64)
            pieces = [slice(c0, c0 + PIECE) for c0 in range(0, HALF, PIECE)]
            grouped = [
                keep.tile([P, PIECE, PACK], BF16, name="grouped%d_%d" % (h, n), align_bytes=64) for n in range(len(pieces))
            ]
            for cols, dst in zip(pieces, grouped):
                nc.vector.tensor_scalar(
                    dst[:].rearrange("p (c i) t -> p c t i", i=4),
                    raw[h][:, :, cols].rearrange("p t (c i) -> p c t i", i=4),
                    -1.0,
                    None,
                    ALU.mult,
                )
            for cols, src in zip(pieces, grouped):
                nc.vector.quantize_mx(
                    out=codes[:, cols].bitcast(FP8X4), scales=plane[:, cols], in_=src[:].rearrange("p c t -> p (c t)")
                )
            rq_codes.append(codes)
            rq_planes.append(plane)

        gate, minus_r, own_term, book, book_term, turned = {}, {}, {}, {}, {}, {}

        def request_side(pair, h, g_width):
            g_acc = psum.tile([P, 2, HALF], F32, name="g_acc", tag=G_BANK[pair, h])
            for c0 in range(0, HALF, g_width):
                cols = slice(c0, c0 + g_width)
                for a in range(2):
                    n0 = (2 * pair + a) * P
                    nc.tensor.matmul_mx(
                        out=g_acc[:, a, cols],
                        lhsT=wg[:, n0 : n0 + P].bitcast(FP8X4),
                        lhsT_scale=wg_plane[:, n0 : n0 + P],
                        rhs=rq_codes[h][:, cols].bitcast(FP8X4),
                        rhs_scale=rq_planes[h][:, cols],
                        start=True,
                        stop=True,
                    )
            r_acc = psum.tile([P, 2, HALF], F32, name="r_acc", tag=R_BANK[pair, h])
            for a in range(2):
                n0 = (2 * pair + a) * P
                nc.tensor.matmul_mx(
                    out=r_acc[:, a, :],
                    lhsT=wr[:, 2 * n0 : 2 * (n0 + P)].bitcast(FP4X4),
                    lhsT_scale=wr_plane[:, n0 : n0 + P],
                    rhs=rq_codes[h][:].bitcast(FP8X4),
                    rhs_scale=rq_planes[h][:],
                    start=True,
                    stop=True,
                )
            s = keep.tile([P, UNIT], F32, name="s%d_%d" % (pair, h), tag="s%d_%d" % (pair, h))
            nc.scalar.activation(s[:], g_acc[:].rearrange("p a j -> p (a j)"), ACT.Sigmoid, scale=-1.0)
            gate[pair, h] = s
            minus_r[pair, h] = r_acc

        def weigh_own(pair, h, tag):
            v = keep.tile([P, UNIT], F32, name="v%d_%d" % (pair, h), tag=tag)
            nc.vector.scalar_tensor_tensor(
                v[:], gate[pair, h][:], 1.0, minus_r[pair, h][:].rearrange("p a j -> p (a j)"), ALU.subtract, ALU.mult
            )
            own_term[pair, h] = v

        def book_side(i):
            z_acc = psum.tile([P, T], F32, name="z_acc", tag=Z_BANK[i])
            a = i % 2
            for z in range(PASSES):
                w_col = (PASSES + z) * N + i * P
                nc.tensor.matmul_mx(
                    out=z_acc[:],
                    lhsT=w[i // 2][:, z, a * P : (a + 1) * P].bitcast(FP8X4),
                    lhsT_scale=book_planes[:, w_col : w_col + P],
                    rhs=xt[:, z, :].bitcast(FP4X4),
                    rhs_scale=book_planes[:, z * T : (z + 1) * T],
                    start=(z == 0),
                    stop=(z == PASSES - 1),
                )
            table = keep.tile([P, T], F32, name="table%d" % i)
            nc.scalar.copy(table[:], z_acc[:])
            book[i] = table

        def look_up(pair, h):
            picked = keep.tile([P, UNIT], F32, name="picked%d_%d" % (pair, h))
            for a in range(2):
                cols = slice(a * HALF, (a + 1) * HALF)
                nc.vector.tensor_tensor(
                    picked[:, cols],
                    book[2 * pair + a][:].indirect(offsets[:, h * HALF // STRIPE : (h + 1) * HALF // STRIPE]),
                    gate[pair, h][:, cols],
                    ALU.mult,
                )
            book_term[pair, h] = picked

        def out_view(pair, h):
            return out[2 * pair * P : 2 * (pair + 1) * P, h * HALF : (h + 1) * HALF].rearrange("(a p) j -> p a j", p=P)

        def add_on_vector(h, a0, a1):
            cols = slice(a0 * HALF, a1 * HALF)
            y = keep.tile([P, a1 - a0, HALF], F32, name="y1_%d_%d" % (h, a0))
            nc.vector.tensor_tensor(
                y[:].rearrange("p a j -> p (a j)"), book_term[1, h][:, cols], own_term[1, h][:, cols], ALU.add
            )
            nc.sync.dma_start(out_view(1, h)[:, a0:a1, :], y[:])

        blocks = [slice(b * P, (b + 1) * P) for b in range(UNIT // P)]

        def add_turned(h):
            turned_acc = psum.tile([P, UNIT], F32, name="turned_acc", tag=TURNED_BANK[h])
            terms = [(term, cols) for term in (own_term[0, h], book_term[0, h]) for cols in blocks]
            for n, (term, cols) in enumerate(terms):
                nc.tensor.matmul(
                    turned_acc[:, cols], term[:, cols], ident[:], start=(n == 0), stop=(n == len(terms) - 1), is_transpose=True
                )
            turned[h] = keep.tile([P, UNIT], F32, name="turned%d" % h)
            nc.scalar.copy(turned[h][:], turned_acc[:])

        def turn_back(h):
            back_acc = psum.tile([P, UNIT], F32, name="back_acc", tag=BACK_BANK[h])
            for cols in blocks:
                nc.tensor.transpose(back_acc[:, cols], turned[h][:, cols], ident[:])
            y = keep.tile([P, 2, HALF], F32, name="y0_%d" % h, tag="v0_%d" % (1 - h))
            nc.scalar.copy(y[:].rearrange("p a j -> p (a j)"), back_acc[:])
            nc.scalar.dma_start(out_view(0, h), y[:])

        quantise(0)
        quantise(1)
        w.append(keep.tile([P, PASSES, 2 * P], U32, name="w1", tag="raw1", align_bytes=64))
        nc.sync.dma_start(w[1][:].bitcast(I32), w_view[:, :, 2 * P : 4 * P])
        for pair, h, g_width in ((0, 0, PIECE), (1, 0, HALF), (0, 1, HALF)):
            request_side(pair, h, g_width)
            weigh_own(pair, h, "v%d_%d" % (pair, h))
        book_side(0)
        book_side(1)
        request_side(1, 1, HALF)
        book_side(2)
        book_side(3)
        for h in range(2):
            look_up(0, h)
            add_turned(h)
        for h in range(2):
            turn_back(h)
        look_up(1, 0)
        weigh_own(1, 1, "s0_1")
        add_on_vector(0, 0, 2)
        look_up(1, 1)
        add_on_vector(1, 0, 1)
        add_on_vector(1, 1, 2)
